import numpy as np
import ml_dtypes


def mxq(x, axis, fmt="e4m3"):
    dtype, down = {"e4m3": (ml_dtypes.float8_e4m3fn, 7), "e5m2": (ml_dtypes.float8_e5m2, 14)}[fmt]
    v = np.moveaxis(np.asarray(x, np.float32).astype(ml_dtypes.bfloat16).astype(np.float64), axis, -1)
    blocks = v.reshape(v.shape[:-1] + (-1, 32))
    amax = np.abs(blocks).max(-1, keepdims=True)
    byte = np.maximum(np.where(amax > 0, np.frexp(amax)[1] - 1 + 127, 0) - down, 1)
    scale = np.exp2(byte - 127.0)
    codes = (blocks / scale).astype(np.float32).astype(dtype).astype(np.float64)
    return np.moveaxis((codes * scale).reshape(v.shape), -1, axis)


WIDE = False


def mx_kscale(k):
    if not WIDE:
        return np.ones(k)
    levels = np.array([10, -10, 5, -5, 0])
    if k % 512:
        return np.exp2(np.random.permutation(np.resize(levels, k // 32))).repeat(32)
    a = np.empty((k // 512, 16))
    for p in range(k // 512):
        a[p, :8] = np.random.permutation(np.resize(levels, 8))
        for g in range(8):
            far = levels[np.abs(levels - a[p, g]) >= 10]
            a[p, g + 8] = far[np.random.randint(len(far))]
    return np.exp2(a.ravel()).repeat(32)


def f64(x):
    return np.asarray(x).astype(np.float64)


E2M1 = np.array([0.0, 0.5, 1.0, 1.5, 2.0, 3.0, 4.0, 6.0, -0.0, -0.5, -1.0, -1.5, -2.0, -3.0, -4.0, -6.0])


def pack_weight(w, fmt):
    k, n = w.shape
    w = f64(np.asarray(w, np.float32).astype(ml_dtypes.bfloat16)).reshape(k // 32, 32, n)
    amax = np.abs(w).max(1)
    if fmt == "e4m3":
        byte = np.frexp(amax)[1] - 1 + 127 - 7
    else:
        mant, ex = np.frexp(amax / 6.0)
        byte = np.where(mant > 0.5, ex, ex - 1) + 127
    byte = np.clip(np.where(amax > 0, byte, 1), 1, 254)
    scaled = (w * np.exp2(127.0 - byte)[:, None, :]).reshape(k, n).astype(np.float32)
    by_word = np.ascontiguousarray(scaled.reshape(k // 512, 128, 4, n).transpose(0, 1, 3, 2))
    if fmt == "e4m3":
        words = by_word.astype(ml_dtypes.float8_e4m3fn).view(np.uint8)
    else:
        c = by_word.astype(ml_dtypes.float4_e2m1fn).view(np.uint8) & 0xF
        words = (c[..., 0::2] | (c[..., 1::2] << 4)).reshape(k // 512, 128, 2 * n)
    return np.ascontiguousarray(words), np.ascontiguousarray(byte.astype(np.uint8).reshape(k // 512, 16, n))


def unpack_weight(words, scales, fmt):
    g, _, n = scales.shape
    words = np.ascontiguousarray(words).reshape(g, 128, n, -1)
    if fmt == "e4m3":
        vals = words.view(ml_dtypes.float8_e4m3fn).astype(np.float64)
    else:
        nib = np.empty((g, 128, n, 4), np.uint8)
        nib[..., 0::2] = words & 0xF
        nib[..., 1::2] = words >> 4
        vals = E2M1[nib]
    vals = vals * np.repeat(np.exp2(scales.astype(np.float64) - 127.0), 8, axis=1)[..., None]
    return vals.transpose(0, 1, 3, 2).reshape(g * 512, n)


def bf(x):
    return np.asarray(x, np.float32).astype(ml_dtypes.bfloat16)


def planes(Y):
    r, m = Y.shape
    b = f64(bf(Y)).reshape(r // 32, 32, m)
    amax = np.abs(b).max(1)
    byte = np.clip(np.where(amax > 0, np.frexp(amax)[1] - 1 + 127 - 7, 1), 1, 254)
    codes = (b * np.exp2(127.0 - byte)[:, None, :]).reshape(r, m).astype(np.float32).astype(ml_dtypes.float8_e4m3fn).view(np.uint8)
    words = codes.reshape(r // 512, 128, 4, m).transpose(0, 1, 3, 2)
    return np.ascontiguousarray(words), np.ascontiguousarray(byte.astype(np.uint8).reshape(r // 512, 16, m))


K, L, Q, I = 512, 1024, 512, 1024


def setup_inputs():
    n = np.random.standard_normal
    fk = mx_kscale(K)
    fl = mx_kscale(L)
    qap = pack_weight(n((K, Q)) * np.random.uniform(0.02, 0.1, (1, Q)) * fk[:, None], "e2m1")
    kap = pack_weight(n((K, I)) / fk[:, None], "e4m3")
    kbp = pack_weight(n((L, I)) / fl[:, None], "e2m1")
    return {
        "qa_words": qap[0],
        "qa_scales": qap[1],
        "ka_words": kap[0],
        "ka_scales": kap[1],
        "qb": (n((L, Q)) * np.random.uniform(0.01, 0.05, (1, Q)) * fl[:, None]).astype(np.float32),
        "kb_words": kbp[0],
        "kb_scales": kbp[1],
        "gn": (np.random.uniform(0.5, 2.0, (1, I))).astype(np.float32),
        "bi": (np.random.uniform(-0.5, 0.5, (1, I))).astype(np.float32),
    }


def reference(qa_words, qa_scales, ka_words, ka_scales, qb, kb_words, kb_scales, gn, bi):
    qau = unpack_weight(qa_words, qa_scales, "e2m1")
    kau = unpack_weight(ka_words, ka_scales, "e4m3")
    kbu = unpack_weight(kb_words, kb_scales, "e2m1")
    qbq = mxq(f64(qb), 0, "e4m3")
    a = qau.T @ kau + qbq.T @ kbu
    d = a - np.mean(a, axis=1, keepdims=True)
    y = d / np.sqrt(np.mean(np.square(d), axis=1, keepdims=True) + 0.02) * f64(gn) + f64(bi)
    words, scales = planes(y)
    return y, words, scales

@@ -1,0 +1,289 @@
+from contextlib import ExitStack
+
+import concourse.mybir as mybir
+from concourse.masks import make_identity
+
+K, L, Q, I = 512, 1024, 512, 1024
+FLOPS = 2 * Q * I * (K + L)
+EPS = 0.02
+
+F32 = mybir.dt.float32
+BF16 = mybir.dt.bfloat16
+I32 = mybir.dt.int32
+U32 = mybir.dt.uint32
+U8 = mybir.dt.uint8
+FP8X4 = mybir.dt.float8_e4m3fn_x4
+FP4X4 = mybir.dt.float4_e2m1fn_x4
+ACT = mybir.ActivationFunctionType
+ALU = mybir.AluOpType
+
+P = 128
+PACK = 4
+K_PASS = P * PACK
+BANK = 512
+HALVES = I // BANK
+B_PASSES = L // K_PASS
+
+
+def tile_mix_scores_of_two_sources_levelled_pl_kernel(
+    tc, qa_words, qa_scales, ka_words, ka_scales, qb, kb_words, kb_scales, gn, bi, out_0, out_1, out_2
+):
+    nc = tc.nc
+    with ExitStack() as ctx:
+        sb = ctx.enter_context(tc.tile_pool(name="sb", bufs=1))
+        ps = ctx.enter_context(tc.psum_pool(name="ps", bufs=1))
+        ctx.enter_context(tc.manual_schedule())
+
+        def tile(name, shape, dtype):
+            return sb.tile(shape, dtype, name=name, align_bytes=64)
+
+        def bank(name, number):
+            return ps.tile([P, BANK], F32, name=name, tag="bank%d" % number)
+
+        def half(h, width=1):
+            return slice(h * BANK * width, (h + 1) * BANK * width)
+
+        def load_scale_rows(plane, scales, quads=range(4)):
+            passes = scales.shape[0]
+            for quad in quads:
+                nc.sync.dma_start(
+                    out=plane[32 * quad : 32 * quad + 4, :].bitcast(I32).rearrange("r (g n) -> r g n", g=passes),
+                    in_=scales[:, 4 * quad : 4 * quad + 4, :].bitcast(I32).rearrange("g r n -> r g n"),
+                )
+
+        kb_plane = tile("kb_plane", [P, B_PASSES * I], U8)
+        ka_plane = tile("ka_plane", [P, I], U8)
+        qa_plane_raw = tile("qa_plane_raw", [P, Q], U8)
+        qa_plane = tile("qa_plane", [P, Q], U8)
+        qa_raw = tile("qa_raw", [P, 2 * Q], U8)
+        qa_codes = tile("qa_codes", [P, 2 * Q], U8)
+        ka_codes = tile("ka_codes", [P, I], U32)
+        kb_codes = [tile("kb_codes%d" % g, [P, 2 * I], U8) for g in range(B_PASSES)]
+        qb_raw = [tile("qb_raw%d" % g, [P, PACK, Q], F32) for g in range(B_PASSES)]
+        qb_bf = [[tile("qb_bf%d_%d" % (g, u), [P, 2, P, PACK], BF16) for u in range(2)] for g in range(B_PASSES)]
+        qb_codes = [[tile("qb_codes%d_%d" % (g, u), [P, 2 * P], U32) for u in range(2)] for g in range(B_PASSES)]
+        qb_plane = [[tile("qb_plane%d_%d" % (g, u), [P, 2 * P], U8) for u in range(2)] for g in range(B_PASSES)]
+        gn_cols = tile("gn_cols", [P, HALVES, 8], F32)
+        bi_cols = tile("bi_cols", [P, HALVES, 8], F32)
+        ident = tile("ident", [P, P], F32)
+        gain = [tile("gain%d" % h, [P, BANK], F32) for h in range(HALVES)]
+        warm = tile("warm", [P, 2], F32)
+
+        nc.vector.memset(kb_plane[:].bitcast(I32), 0)
+        nc.vector.memset(qa_plane_raw[:].bitcast(I32), 0)
+        nc.vector.memset(ka_plane[:].bitcast(I32), 0)
+        nc.vector.memset(warm[:, 0:1], 1.0)
+        nc.scalar.activation(out=warm[:, 1:2], in_=warm[:, 0:1], func=ACT.Abs_reciprocal_sqrt)
+
+        def load_qb(g):
+            rows = qb[g * K_PASS : (g + 1) * K_PASS, :]
+            nc.sync.dma_start(out=qb_raw[g][:], in_=rows.rearrange("(p j) w -> p j w", j=PACK))
+
+        def load_kb(g):
+            nc.sync.dma_start(out=kb_codes[g][:].bitcast(I32), in_=kb_words[g].bitcast(I32))
+
+        load_qb(0)
+        load_scale_rows(kb_plane, kb_scales)
+        load_kb(0)
+        nc.sync.dma_start(out=qa_raw[:].bitcast(I32), in_=qa_words[0].bitcast(I32))
+        load_qb(1)
+        load_scale_rows(qa_plane_raw, qa_scales)
+        load_scale_rows(ka_plane, ka_scales, (0, 1))
+        nc.sync.dma_start(out=ka_codes[:].bitcast(I32), in_=ka_words[0].rearrange("p n t -> p (n t)").bitcast(I32))
+        load_scale_rows(ka_plane, ka_scales, (2, 3))
+        load_kb(1)
+
+        for cols, vec in ((gn_cols, gn), (bi_cols, bi)):
+            nc.gpsimd.dma_start(out=cols[:, :, 0:4], in_=vec[0].rearrange("(h n c) -> n h c", h=HALVES, c=4))
+        make_identity(nc, ident[:])
+
+        def spread(cols, name):
+            banks = []
+            for h in range(HALVES):
+                spread_bank = bank("%s%d" % (name, h), 6 + h)
+                for c in range(4):
+                    nc.tensor.transpose(
+                        spread_bank[:, c * P : (c + 1) * P], cols[:, h, c : c + 1].to_broadcast([P, P]), ident[:]
+                    )
+                banks.append(spread_bank)
+            return banks
+
+        def in_order(spread_bank):
+            return spread_bank[:].rearrange("p (c n) -> p n c", c=4)
+
+        def round_qb(g, u):
+            dst = qb_bf[g][u][:].rearrange("p r m j -> p m j r")
+            src = qb_raw[g][:].rearrange("p j (m r) -> p m j r", r=PACK)[:, :, :, 2 * u : 2 * u + 2]
+            if u == 0:
+                nc.vector.tensor_copy(out=dst, in_=src)
+            else:
+                nc.scalar.copy(out=dst, in_=src)
+
+        def quantize_qb(g, u):
+            nc.vector.quantize_mx(
+                out=qb_codes[g][u][:].bitcast(FP8X4),
+                scales=qb_plane[g][u][:],
+                in_=qb_bf[g][u][:].rearrange("p r m j -> p (r m j)"),
+            )
+
+        acc = {}
+
+        def pass_a(r, start, stop):
+            for h in range(HALVES):
+                nc.tensor.matmul_mx(
+                    out=acc[r, h][:],
+                    lhsT=qa_codes[:, 2 * P * r : 2 * P * (r + 1)].bitcast(FP4X4),
+                    lhsT_scale=qa_plane[:, P * r : P * (r + 1)],
+                    rhs=ka_codes[:, half(h)].bitcast(FP8X4),
+                    rhs_scale=ka_plane[:, half(h)],
+                    start=start,
+                    stop=stop,
+                )
+
+        def pass_b(g, r, start, stop):
+            cols = slice(P * (r % 2), P * (r % 2 + 1))
+            for h in range(HALVES):
+                nc.tensor.matmul_mx(
+                    out=acc[r, h][:],
+                    lhsT=qb_codes[g][r // 2][:, cols].bitcast(FP8X4),
+                    lhsT_scale=qb_plane[g][r // 2][:, cols],
+                    rhs=kb_codes[g][:, half(h, 2)].bitcast(FP4X4),
+                    rhs_scale=kb_plane[:, g * I + h * BANK : g * I + (h + 1) * BANK],
+                    start=start,
+                    stop=stop,
+                )
+
+        gain_banks = spread(gn_cols, "gain_bank")
+        round_qb(0, 0)
+        round_qb(0, 1)
+        quantize_qb(0, 0)
+        nc.vector.tensor_copy(
+            out=qa_codes[:].rearrange("p (r m b) -> p m r b", r=PACK, b=2),
+            in_=qa_raw[:].rearrange("p (m r b) -> p m r b", r=PACK, b=2),
+        )
+        quantize_qb(0, 1)
+        for h in range(HALVES):
+            nc.scalar.copy(out=gain[h][:].rearrange("p (n c) -> p n c", c=4), in_=in_order(gain_banks[h]))
+        for r in range(3):
+            for h in range(HALVES):
+                acc[r, h] = bank("acc%d_%d" % (r, h), 2 * r + h)
+            pass_b(0, r, True, False)
+        bias_banks = spread(bi_cols, "bias_bank")
+        round_qb(1, 0)
+        round_qb(1, 1)
+        nc.vector.tensor_copy(
+            out=qa_plane[:].rearrange("p (r m) -> p m r", r=PACK),
+            in_=qa_plane_raw[:].rearrange("p (m r) -> p m r", r=PACK),
+        )
+        quantize_qb(1, 0)
+        quantize_qb(1, 1)
+        pass_a(0, False, False)
+        pass_a(1, False, False)
+        pass_b(1, 0, False, True)
+        pass_b(1, 1, False, True)
+        pass_a(2, False, False)
+        pass_b(1, 2, False, True)
+
+        y = [tile("y%d" % h, [P, PACK, BANK], F32) for h in range(HALVES)]
+        centred = {(r, h): tile("centred%d_%d" % (r, h), [P, BANK], F32) for r in range(PACK) for h in range(HALVES)}
+        shrunk = {r: tile("shrunk%d" % r, [P, I], F32) for r in range(1, PACK)}
+        squares = tile("squares", [P, I], BF16)
+        part = {(r, h): tile("part%d_%d" % (r, h), [P, 1], F32) for r in range(1, PACK) for h in range(HALVES)}
+        neg_mean = {r: tile("neg_mean%d" % r, [P, 1], F32) for r in range(1, PACK)}
+        sum_sq = {r: tile("sum_sq%d" % r, [P, 1], F32) for r in range(1, PACK)}
+        rstd = {r: tile("rstd%d" % r, [P, 1], F32) for r in range(PACK)}
+        stats = tile("stats", [P, HALVES * 6], F32)
+        mean_var = tile("mean_var", [P, 2], F32)
+        out_rows = out_0.rearrange("(p r) i -> p r i", r=PACK)
+
+        def sum_half(r, h):
+            nc.scalar.activation(
+                out=shrunk[r][:, half(h)], in_=acc[r, h][:], func=ACT.Copy, scale=-1.0 / I, accum_out=part[r, h][:]
+            )
+
+        def join_mean(r):
+            nc.scalar.activation(out=neg_mean[r][:], in_=part[r, 0][:], func=ACT.Identity, bias=part[r, 1][:])
+
+        def sum_squares(r):
+            nc.scalar.activation(
+                out=squares[:], in_=shrunk[r][:], func=ACT.Square, scale=-float(I), bias=neg_mean[r][:],
+                accum_out=sum_sq[r][:],
+            )
+
+        def inverse_spread(r):
+            if r == 0:
+                nc.scalar.activation(out=rstd[0][:], in_=mean_var[:, 1:2], func=ACT.Abs_reciprocal_sqrt, bias=EPS)
+            else:
+                nc.scalar.activation(
+                    out=rstd[r][:], in_=sum_sq[r][:], func=ACT.Abs_reciprocal_sqrt, scale=1.0 / I, bias=EPS
+                )
+
+        def centre(r, h):
+            shift, op = (mean_var[:, 0:1], ALU.subtract) if r == 0 else (neg_mean[r][:], ALU.add)
+            nc.vector.scalar_tensor_tensor(
+                out=centred[r, h][:], in0=acc[r, h][:], scalar=shift, in1=gain[h][:], op0=op, op1=ALU.mult
+            )
+
+        def finish(r, h):
+            nc.vector.scalar_tensor_tensor(
+                out=y[h][:, r, :].rearrange("p (n c) -> p n c", c=4),
+                in0=centred[r, h][:].rearrange("p (n c) -> p n c", c=4),
+                scalar=rstd[r][:],
+                in1=in_order(bias_banks[h]),
+                op0=ALU.mult,
+                op1=ALU.add,
+            )
+            nc.sync.dma_start(out=out_rows[:, r, half(h)], in_=y[h][:, r, :])
+
+        for h in range(HALVES):
+            nc.vector.bn_stats(out=stats[:, 6 * h : 6 * h + 6], in_=acc[0, h][:])
+        nc.vector.bn_aggr(out=mean_var[:], in_=stats[:])
+        sum_half(1, 0)
+        sum_half(1, 1)
+        join_mean(1)
+        inverse_spread(0)
+        for h in range(HALVES):
+            centre(0, h)
+        for h in range(HALVES):
+            acc[3, h] = bank("acc3_%d" % h, h)
+        pass_b(0, 3, True, False)
+        pass_a(3, False, False)
+        pass_b(1, 3, False, True)
+        for h in range(HALVES):
+            finish(0, h)
+        for r in range(1, PACK):
+            sum_squares(r)
+            if r + 1 < PACK:
+                sum_half(r + 1, 0)
+            inverse_spread(r)
+            if r + 1 < PACK:
+                sum_half(r + 1, 1)
+                join_mean(r + 1)
+            for h in range(HALVES):
+                centre(r, h)
+            for h in range(HALVES):
+                finish(r, h)
+
+        y_bf = [tile("y_bf%d" % h, [P, BANK, PACK], BF16) for h in range(HALVES)]
+        y_codes = [tile("y_codes%d" % h, [P, BANK], U32) for h in range(HALVES)]
+        y_plane = tile("y_plane", [P, I], U8)
+        words_out = out_1[0].rearrange("p n t -> p (n t)").bitcast(I32)
+        for h in range(HALVES):
+            dst = y_bf[h][:].rearrange("p (c i) r -> p c r i", i=4)
+            src = y[h][:].rearrange("p r (c i) -> p c r i", i=4)
+            if h == 0:
+                nc.scalar.copy(out=dst, in_=src)
+            else:
+                nc.vector.tensor_copy(out=dst, in_=src)
+        for h in reversed(range(HALVES)):
+            nc.vector.quantize_mx(
+                out=y_codes[h][:].bitcast(FP8X4),
+                scales=y_plane[:, half(h)],
+                in_=y_bf[h][:].rearrange("p n r -> p (n r)"),
+            )
+            nc.sync.dma_start(out=words_out[:, half(h)], in_=y_codes[h][:].bitcast(I32))
+        for quad in range(4):
+            nc.scalar.dma_start(
+                out=out_2[0, 4 * quad : 4 * quad + 4, :].bitcast(I32),
+                in_=y_plane[32 * quad : 32 * quad + 4, :].bitcast(I32),
+            )

@@ -43,10 +43,10 @@ def tile_mix_scores_of_two_sources_levelled_pl_kernel(
         def half(h, width=1):
             return slice(h * BANK * width, (h + 1) * BANK * width)
 
-        def load_scale_rows(plane, scales, quads=range(4)):
+        def load_scale_rows(plane, scales, queue=nc.sync):
             passes = scales.shape[0]
-            for quad in quads:
-                nc.sync.dma_start(
+            for quad in range(4):
+                queue.dma_start(
                     out=plane[32 * quad : 32 * quad + 4, :].bitcast(I32).rearrange("r (g n) -> r g n", g=passes),
                     in_=scales[:, 4 * quad : 4 * quad + 4, :].bitcast(I32).rearrange("g r n -> r g n"),
                 )
@@ -70,8 +70,8 @@ def tile_mix_scores_of_two_sources_levelled_pl_kernel(
         warm = tile("warm", [P, 2], F32)
 
         nc.vector.memset(kb_plane[:].bitcast(I32), 0)
-        nc.vector.memset(qa_plane_raw[:].bitcast(I32), 0)
         nc.vector.memset(ka_plane[:].bitcast(I32), 0)
+        nc.vector.memset(qa_plane_raw[:].bitcast(I32), 0)
         nc.vector.memset(warm[:, 0:1], 1.0)
         nc.scalar.activation(out=warm[:, 1:2], in_=warm[:, 0:1], func=ACT.Abs_reciprocal_sqrt)
 
@@ -82,20 +82,22 @@ def tile_mix_scores_of_two_sources_levelled_pl_kernel(
         def load_kb(g):
             nc.sync.dma_start(out=kb_codes[g][:].bitcast(I32), in_=kb_words[g].bitcast(I32))
 
+        def load_columns(cols, vec):
+            nc.sync.dma_start(out=cols[:, :, 0:4], in_=vec[0].rearrange("(h n c) -> n h c", h=HALVES, c=4))
+
         load_qb(0)
+        nc.sync.dma_start(out=qa_raw[:].bitcast(I32), in_=qa_words[0].bitcast(I32))
         load_scale_rows(kb_plane, kb_scales)
         load_kb(0)
-        nc.sync.dma_start(out=qa_raw[:].bitcast(I32), in_=qa_words[0].bitcast(I32))
         load_qb(1)
+        load_columns(gn_cols, gn)
         load_scale_rows(qa_plane_raw, qa_scales)
-        load_scale_rows(ka_plane, ka_scales, (0, 1))
         nc.sync.dma_start(out=ka_codes[:].bitcast(I32), in_=ka_words[0].rearrange("p n t -> p (n t)").bitcast(I32))
-        load_scale_rows(ka_plane, ka_scales, (2, 3))
         load_kb(1)
+        load_columns(bi_cols, bi)
 
-        for cols, vec in ((gn_cols, gn), (bi_cols, bi)):
-            nc.gpsimd.dma_start(out=cols[:, :, 0:4], in_=vec[0].rearrange("(h n c) -> n h c", h=HALVES, c=4))
         make_identity(nc, ident[:])
+        load_scale_rows(ka_plane, ka_scales, nc.gpsimd)
 
         def spread(cols, name):
             banks = []
@@ -153,34 +155,35 @@ def tile_mix_scores_of_two_sources_levelled_pl_kernel(
                     stop=stop,
                 )
 
-        gain_banks = spread(gn_cols, "gain_bank")
         round_qb(0, 0)
         round_qb(0, 1)
         quantize_qb(0, 0)
         nc.vector.tensor_copy(
-            out=qa_codes[:].rearrange("p (r m b) -> p m r b", r=PACK, b=2),
-            in_=qa_raw[:].rearrange("p (m r b) -> p m r b", r=PACK, b=2),
+            out=qa_codes[:].rearrange("p (r m b) -> p r m b", r=PACK, b=2),
+            in_=qa_raw[:].rearrange("p (m r b) -> p r m b", r=PACK, b=2),
         )
         quantize_qb(0, 1)
-        for h in range(HALVES):
-            nc.scalar.copy(out=gain[h][:].rearrange("p (n c) -> p n c", c=4), in_=in_order(gain_banks[h]))
         for r in range(3):
             for h in range(HALVES):
                 acc[r, h] = bank("acc%d_%d" % (r, h), 2 * r + h)
-            pass_b(0, r, True, False)
-        bias_banks = spread(bi_cols, "bias_bank")
+        pass_b(0, 0, True, False)
+        pass_b(0, 1, True, False)
+        gain_banks = spread(gn_cols, "gain_bank")
         round_qb(1, 0)
         round_qb(1, 1)
         nc.vector.tensor_copy(
-            out=qa_plane[:].rearrange("p (r m) -> p m r", r=PACK),
-            in_=qa_plane_raw[:].rearrange("p (m r) -> p m r", r=PACK),
+            out=qa_plane[:].rearrange("p (r m) -> p r m", r=PACK),
+            in_=qa_plane_raw[:].rearrange("p (m r) -> p r m", r=PACK),
         )
         quantize_qb(1, 0)
         quantize_qb(1, 1)
-        pass_a(0, False, False)
-        pass_a(1, False, False)
-        pass_b(1, 0, False, True)
-        pass_b(1, 1, False, True)
+        for h in range(HALVES):
+            nc.scalar.copy(out=gain[h][:].rearrange("p (n c) -> p n c", c=4), in_=in_order(gain_banks[h]))
+        for r in range(2):
+            pass_a(r, False, False)
+            pass_b(1, r, False, True)
+        bias_banks = spread(bi_cols, "bias_bank")
+        pass_b(0, 2, True, False)
         pass_a(2, False, False)
         pass_b(1, 2, False, True)
 

from contextlib import ExitStack

import concourse.mybir as mybir
from concourse.masks import make_identity

K, L, Q, I = 512, 1024, 512, 1024
FLOPS = 2 * Q * I * (K + L)
EPS = 0.02

F32 = mybir.dt.float32
BF16 = mybir.dt.bfloat16
I32 = mybir.dt.int32
U32 = mybir.dt.uint32
U8 = mybir.dt.uint8
FP8X4 = mybir.dt.float8_e4m3fn_x4
FP4X4 = mybir.dt.float4_e2m1fn_x4
ACT = mybir.ActivationFunctionType
ALU = mybir.AluOpType

P = 128
PACK = 4
K_PASS = P * PACK
BANK = 512
HALVES = I // BANK
B_PASSES = L // K_PASS


def tile_mix_scores_of_two_sources_levelled_pl_kernel(
    tc, qa_words, qa_scales, ka_words, ka_scales, qb, kb_words, kb_scales, gn, bi, out_0, out_1, out_2
):
    nc = tc.nc
    with ExitStack() as ctx:
        sb = ctx.enter_context(tc.tile_pool(name="sb", bufs=1))
        ps = ctx.enter_context(tc.psum_pool(name="ps", bufs=1))
        ctx.enter_context(tc.manual_schedule())

        def tile(name, shape, dtype):
            return sb.tile(shape, dtype, name=name, align_bytes=64)

        def bank(name, number):
            return ps.tile([P, BANK], F32, name=name, tag="bank%d" % number)

        def half(h, width=1):
            return slice(h * BANK * width, (h + 1) * BANK * width)

        def load_scale_rows(plane, scales, queue=nc.sync):
            passes = scales.shape[0]
            for quad in range(4):
                queue.dma_start(
                    out=plane[32 * quad : 32 * quad + 4, :].bitcast(I32).rearrange("r (g n) -> r g n", g=passes),
                    in_=scales[:, 4 * quad : 4 * quad + 4, :].bitcast(I32).rearrange("g r n -> r g n"),
                )

        kb_plane = tile("kb_plane", [P, B_PASSES * I], U8)
        ka_plane = tile("ka_plane", [P, I], U8)
        qa_plane_raw = tile("qa_plane_raw", [P, Q], U8)
        qa_plane = tile("qa_plane", [P, Q], U8)
        qa_raw = tile("qa_raw", [P, 2 * Q], U8)
        qa_codes = tile("qa_codes", [P, 2 * Q], U8)
        ka_codes = tile("ka_codes", [P, I], U32)
        kb_codes = [tile("kb_codes%d" % g, [P, 2 * I], U8) for g in range(B_PASSES)]
        qb_raw = [tile("qb_raw%d" % g, [P, PACK, Q], F32) for g in range(B_PASSES)]
        qb_bf = [[tile("qb_bf%d_%d" % (g, u), [P, 2, P, PACK], BF16) for u in range(2)] for g in range(B_PASSES)]
        qb_codes = [[tile("qb_codes%d_%d" % (g, u), [P, 2 * P], U32) for u in range(2)] for g in range(B_PASSES)]
        qb_plane = [[tile("qb_plane%d_%d" % (g, u), [P, 2 * P], U8) for u in range(2)] for g in range(B_PASSES)]
        gn_cols = tile("gn_cols", [P, HALVES, 8], F32)
        bi_cols = tile("bi_cols", [P, HALVES, 8], F32)
        ident = tile("ident", [P, P], F32)
        gain = [tile("gain%d" % h, [P, BANK], F32) for h in range(HALVES)]
        warm = tile("warm", [P, 2], F32)

        nc.vector.memset(kb_plane[:].bitcast(I32), 0)
        nc.vector.memset(ka_plane[:].bitcast(I32), 0)
        nc.vector.memset(qa_plane_raw[:].bitcast(I32), 0)
        nc.vector.memset(warm[:, 0:1], 1.0)
        nc.scalar.activation(out=warm[:, 1:2], in_=warm[:, 0:1], func=ACT.Abs_reciprocal_sqrt)

        def load_qb(g):
            rows = qb[g * K_PASS : (g + 1) * K_PASS, :]
            nc.sync.dma_start(out=qb_raw[g][:], in_=rows.rearrange("(p j) w -> p j w", j=PACK))

        def load_kb(g):
            nc.sync.dma_start(out=kb_codes[g][:].bitcast(I32), in_=kb_words[g].bitcast(I32))

        def load_columns(cols, vec):
            nc.sync.dma_start(out=cols[:, :, 0:4], in_=vec[0].rearrange("(h n c) -> n h c", h=HALVES, c=4))

        load_qb(0)
        nc.sync.dma_start(out=qa_raw[:].bitcast(I32), in_=qa_words[0].bitcast(I32))
        load_scale_rows(kb_plane, kb_scales)
        load_kb(0)
        load_qb(1)
        load_columns(gn_cols, gn)
        load_scale_rows(qa_plane_raw, qa_scales)
        nc.sync.dma_start(out=ka_codes[:].bitcast(I32), in_=ka_words[0].rearrange("p n t -> p (n t)").bitcast(I32))
        load_kb(1)
        load_columns(bi_cols, bi)

        make_identity(nc, ident[:])
        load_scale_rows(ka_plane, ka_scales, nc.gpsimd)

        def spread(cols, name):
            banks = []
            for h in range(HALVES):
                spread_bank = bank("%s%d" % (name, h), 6 + h)
                for c in range(4):
                    nc.tensor.transpose(
                        spread_bank[:, c * P : (c + 1) * P], cols[:, h, c : c + 1].to_broadcast([P, P]), ident[:]
                    )
                banks.append(spread_bank)
            return banks

        def in_order(spread_bank):
            return spread_bank[:].rearrange("p (c n) -> p n c", c=4)

        def round_qb(g, u):
            dst = qb_bf[g][u][:].rearrange("p r m j -> p m j r")
            src = qb_raw[g][:].rearrange("p j (m r) -> p m j r", r=PACK)[:, :, :, 2 * u : 2 * u + 2]
            if u == 0:
                nc.vector.tensor_copy(out=dst, in_=src)
            else:
                nc.scalar.copy(out=dst, in_=src)

        def quantize_qb(g, u):
            nc.vector.quantize_mx(
                out=qb_codes[g][u][:].bitcast(FP8X4),
                scales=qb_plane[g][u][:],
                in_=qb_bf[g][u][:].rearrange("p r m j -> p (r m j)"),
            )

        acc = {}

        def pass_a(r, start, stop):
            for h in range(HALVES):
                nc.tensor.matmul_mx(
                    out=acc[r, h][:],
                    lhsT=qa_codes[:, 2 * P * r : 2 * P * (r + 1)].bitcast(FP4X4),
                    lhsT_scale=qa_plane[:, P * r : P * (r + 1)],
                    rhs=ka_codes[:, half(h)].bitcast(FP8X4),
                    rhs_scale=ka_plane[:, half(h)],
                    start=start,
                    stop=stop,
                )

        def pass_b(g, r, start, stop):
            cols = slice(P * (r % 2), P * (r % 2 + 1))
            for h in range(HALVES):
                nc.tensor.matmul_mx(
                    out=acc[r, h][:],
                    lhsT=qb_codes[g][r // 2][:, cols].bitcast(FP8X4),
                    lhsT_scale=qb_plane[g][r // 2][:, cols],
                    rhs=kb_codes[g][:, half(h, 2)].bitcast(FP4X4),
                    rhs_scale=kb_plane[:, g * I + h * BANK : g * I + (h + 1) * BANK],
                    start=start,
                    stop=stop,
                )

        round_qb(0, 0)
        round_qb(0, 1)
        quantize_qb(0, 0)
        nc.vector.tensor_copy(
            out=qa_codes[:].rearrange("p (r m b) -> p r m b", r=PACK, b=2),
            in_=qa_raw[:].rearrange("p (m r b) -> p r m b", r=PACK, b=2),
        )
        quantize_qb(0, 1)
        for r in range(3):
            for h in range(HALVES):
                acc[r, h] = bank("acc%d_%d" % (r, h), 2 * r + h)
        pass_b(0, 0, True, False)
        pass_b(0, 1, True, False)
        gain_banks = spread(gn_cols, "gain_bank")
        round_qb(1, 0)
        round_qb(1, 1)
        nc.vector.tensor_copy(
            out=qa_plane[:].rearrange("p (r m) -> p r m", r=PACK),
            in_=qa_plane_raw[:].rearrange("p (m r) -> p r m", r=PACK),
        )
        quantize_qb(1, 0)
        quantize_qb(1, 1)
        for h in range(HALVES):
            nc.scalar.copy(out=gain[h][:].rearrange("p (n c) -> p n c", c=4), in_=in_order(gain_banks[h]))
        for r in range(2):
            pass_a(r, False, False)
            pass_b(1, r, False, True)
        bias_banks = spread(bi_cols, "bias_bank")
        pass_b(0, 2, True, False)
        pass_a(2, False, False)
        pass_b(1, 2, False, True)

        y = [tile("y%d" % h, [P, PACK, BANK], F32) for h in range(HALVES)]
        centred = {(r, h): tile("centred%d_%d" % (r, h), [P, BANK], F32) for r in range(PACK) for h in range(HALVES)}
        shrunk = {r: tile("shrunk%d" % r, [P, I], F32) for r in range(1, PACK)}
        squares = tile("squares", [P, I], BF16)
        part = {(r, h): tile("part%d_%d" % (r, h), [P, 1], F32) for r in range(1, PACK) for h in range(HALVES)}
        neg_mean = {r: tile("neg_mean%d" % r, [P, 1], F32) for r in range(1, PACK)}
        sum_sq = {r: tile("sum_sq%d" % r, [P, 1], F32) for r in range(1, PACK)}
        rstd = {r: tile("rstd%d" % r, [P, 1], F32) for r in range(PACK)}
        stats = tile("stats", [P, HALVES * 6], F32)
        mean_var = tile("mean_var", [P, 2], F32)
        out_rows = out_0.rearrange("(p r) i -> p r i", r=PACK)

        def sum_half(r, h):
            nc.scalar.activation(
                out=shrunk[r][:, half(h)], in_=acc[r, h][:], func=ACT.Copy, scale=-1.0 / I, accum_out=part[r, h][:]
            )

        def join_mean(r):
            nc.scalar.activation(out=neg_mean[r][:], in_=part[r, 0][:], func=ACT.Identity, bias=part[r, 1][:])

        def sum_squares(r):
            nc.scalar.activation(
                out=squares[:], in_=shrunk[r][:], func=ACT.Square, scale=-float(I), bias=neg_mean[r][:],
                accum_out=sum_sq[r][:],
            )

        def inverse_spread(r):
            if r == 0:
                nc.scalar.activation(out=rstd[0][:], in_=mean_var[:, 1:2], func=ACT.Abs_reciprocal_sqrt, bias=EPS)
            else:
                nc.scalar.activation(
                    out=rstd[r][:], in_=sum_sq[r][:], func=ACT.Abs_reciprocal_sqrt, scale=1.0 / I, bias=EPS
                )

        def centre(r, h):
            shift, op = (mean_var[:, 0:1], ALU.subtract) if r == 0 else (neg_mean[r][:], ALU.add)
            nc.vector.scalar_tensor_tensor(
                out=centred[r, h][:], in0=acc[r, h][:], scalar=shift, in1=gain[h][:], op0=op, op1=ALU.mult
            )

        def finish(r, h):
            nc.vector.scalar_tensor_tensor(
                out=y[h][:, r, :].rearrange("p (n c) -> p n c", c=4),
                in0=centred[r, h][:].rearrange("p (n c) -> p n c", c=4),
                scalar=rstd[r][:],
                in1=in_order(bias_banks[h]),
                op0=ALU.mult,
                op1=ALU.add,
            )
            nc.sync.dma_start(out=out_rows[:, r, half(h)], in_=y[h][:, r, :])

        for h in range(HALVES):
            nc.vector.bn_stats(out=stats[:, 6 * h : 6 * h + 6], in_=acc[0, h][:])
        nc.vector.bn_aggr(out=mean_var[:], in_=stats[:])
        sum_half(1, 0)
        sum_half(1, 1)
        join_mean(1)
        inverse_spread(0)
        for h in range(HALVES):
            centre(0, h)
        for h in range(HALVES):
            acc[3, h] = bank("acc3_%d" % h, h)
        pass_b(0, 3, True, False)
        pass_a(3, False, False)
        pass_b(1, 3, False, True)
        for h in range(HALVES):
            finish(0, h)
        for r in range(1, PACK):
            sum_squares(r)
            if r + 1 < PACK:
                sum_half(r + 1, 0)
            inverse_spread(r)
            if r + 1 < PACK:
                sum_half(r + 1, 1)
                join_mean(r + 1)
            for h in range(HALVES):
                centre(r, h)
            for h in range(HALVES):
                finish(r, h)

        y_bf = [tile("y_bf%d" % h, [P, BANK, PACK], BF16) for h in range(HALVES)]
        y_codes = [tile("y_codes%d" % h, [P, BANK], U32) for h in range(HALVES)]
        y_plane = tile("y_plane", [P, I], U8)
        words_out = out_1[0].rearrange("p n t -> p (n t)").bitcast(I32)
        for h in range(HALVES):
            dst = y_bf[h][:].rearrange("p (c i) r -> p c r i", i=4)
            src = y[h][:].rearrange("p r (c i) -> p c r i", i=4)
            if h == 0:
                nc.scalar.copy(out=dst, in_=src)
            else:
                nc.vector.tensor_copy(out=dst, in_=src)
        for h in reversed(range(HALVES)):
            nc.vector.quantize_mx(
                out=y_codes[h][:].bitcast(FP8X4),
                scales=y_plane[:, half(h)],
                in_=y_bf[h][:].rearrange("p n r -> p (n r)"),
            )
            nc.sync.dma_start(out=words_out[:, half(h)], in_=y_codes[h][:].bitcast(I32))
        for quad in range(4):
            nc.scalar.dma_start(
                out=out_2[0, 4 * quad : 4 * quad + 4, :].bitcast(I32),
                in_=y_plane[32 * quad : 32 * quad + 4, :].bitcast(I32),
            )
